import numpy as np
import ml_dtypes


def mxq(x, axis, fmt="e4m3"):
    dtype, down = {"e4m3": (ml_dtypes.float8_e4m3fn, 7), "e5m2": (ml_dtypes.float8_e5m2, 14)}[fmt]
    v = np.moveaxis(np.asarray(x, np.float32).astype(ml_dtypes.bfloat16).astype(np.float64), axis, -1)
    blocks = v.reshape(v.shape[:-1] + (-1, 32))
    amax = np.abs(blocks).max(-1, keepdims=True)
    byte = np.maximum(np.where(amax > 0, np.frexp(amax)[1] - 1 + 127, 0) - down, 1)
    scale = np.exp2(byte - 127.0)
    codes = (blocks / scale).astype(np.float32).astype(dtype).astype(np.float64)
    return np.moveaxis((codes * scale).reshape(v.shape), -1, axis)


WIDE = False


def mx_kscale(k):
    if not WIDE:
        return np.ones(k)
    levels = np.array([10, -10, 5, -5, 0])
    if k % 512:
        return np.exp2(np.random.permutation(np.resize(levels, k // 32))).repeat(32)
    a = np.empty((k // 512, 16))
    for p in range(k // 512):
        a[p, :8] = np.random.permutation(np.resize(levels, 8))
        for g in range(8):
            far = levels[np.abs(levels - a[p, g]) >= 10]
            a[p, g + 8] = far[np.random.randint(len(far))]
    return np.exp2(a.ravel()).repeat(32)


def f64(x):
    return np.asarray(x).astype(np.float64)


def striped(idx):
    return np.tile(idx.reshape(-1, 16).T, (8, 1)).astype(np.uint16)


def unstriped(offs):
    return offs[:16].T.reshape(-1).astype(np.int64)


E2M1 = np.array([0.0, 0.5, 1.0, 1.5, 2.0, 3.0, 4.0, 6.0, -0.0, -0.5, -1.0, -1.5, -2.0, -3.0, -4.0, -6.0])


def pack_weight(w, fmt):
    k, n = w.shape
    w = f64(np.asarray(w, np.float32).astype(ml_dtypes.bfloat16)).reshape(k // 32, 32, n)
    amax = np.abs(w).max(1)
    if fmt == "e4m3":
        byte = np.frexp(amax)[1] - 1 + 127 - 7
    else:
        mant, ex = np.frexp(amax / 6.0)
        byte = np.where(mant > 0.5, ex, ex - 1) + 127
    byte = np.clip(np.where(amax > 0, byte, 1), 1, 254)
    scaled = (w * np.exp2(127.0 - byte)[:, None, :]).reshape(k, n).astype(np.float32)
    by_word = np.ascontiguousarray(scaled.reshape(k // 512, 128, 4, n).transpose(0, 1, 3, 2))
    if fmt == "e4m3":
        words = by_word.astype(ml_dtypes.float8_e4m3fn).view(np.uint8)
    else:
        c = by_word.astype(ml_dtypes.float4_e2m1fn).view(np.uint8) & 0xF
        words = (c[..., 0::2] | (c[..., 1::2] << 4)).reshape(k // 512, 128, 2 * n)
    return np.ascontiguousarray(words), np.ascontiguousarray(byte.astype(np.uint8).reshape(k // 512, 16, n))


def unpack_weight(words, scales, fmt):
    g, _, n = scales.shape
    words = np.ascontiguousarray(words).reshape(g, 128, n, -1)
    if fmt == "e4m3":
        vals = words.view(ml_dtypes.float8_e4m3fn).astype(np.float64)
    else:
        nib = np.empty((g, 128, n, 4), np.uint8)
        nib[..., 0::2] = words & 0xF
        nib[..., 1::2] = words >> 4
        vals = E2M1[nib]
    vals = vals * np.repeat(np.exp2(scales.astype(np.float64) - 127.0), 8, axis=1)[..., None]
    return vals.transpose(0, 1, 3, 2).reshape(g * 512, n)


def d_relu2(v):
    return 2.0 * np.maximum(v, 0.0)


K, T, E, C, H, N = 512, 768, 6, 256, 512, 1024


def by_expert(wq, xq):
    return np.concatenate([wq[e].T @ xq[:, e * C:(e + 1) * C] for e in range(E)], axis=1)


def setup_inputs():
    n = np.random.standard_normal
    s = mx_kscale(N)[:, None]
    u = mx_kscale(H)
    first = np.random.permutation(np.repeat(np.arange(E), T // E))
    second = (first + 1 + np.random.permutation(np.repeat(np.arange(E - 1), -(-T // (E - 1)))[:T])) % E
    while np.bincount(second, minlength=E).max() != T // E:
        load = np.bincount(second, minlength=E); hi, lo = int(load.argmax()), int(load.argmin())
        t = np.flatnonzero((second == hi) & (first != lo))[0]; second[t] = lo
    slot_token = np.empty(E * C, np.int64); pos = np.empty((2, T), np.int64); fill = np.zeros(E, np.int64)
    place = np.stack([np.random.permutation(C) for _ in range(E)])
    for r, deal in enumerate((first, second)):
        for t in np.random.permutation(T):
            e = deal[t]; j = e * C + place[e, fill[e]]; fill[e] += 1; slot_token[j] = t; pos[r, t] = j
    g = np.random.uniform(0.2, 0.8, T)
    w_slot = np.empty(E * C); w_slot[pos[0]] = g; w_slot[pos[1]] = 1.0 - g
    w2 = [pack_weight(m, "e2m1") for m in n((E, N, H)) / np.sqrt(N) / s[None] * u[None, None, :]]
    w1 = [pack_weight(m, "e2m1") for m in n((E, H, K)) / np.sqrt(H) / u[None, :, None]]
    return {
        "dyT": (n((N, T)) * s).astype(np.float32),
        "a": n((H, E * C)).astype(np.float32),
        "w2_words": np.stack([m[0] for m in w2]),
        "w2_scales": np.stack([m[1] for m in w2]),
        "w1_words": np.stack([m[0] for m in w1]),
        "w1_scales": np.stack([m[1] for m in w1]),
        "gate": np.tile(w_slot, (N, 1)).astype(np.float32),
        "offs": striped(slot_token),
        "pos1": striped(pos[0]),
        "pos2": striped(pos[1]),
    }


def reference(dyT, a, w2_words, w2_scales, w1_words, w1_scales, gate, offs, pos1, pos2):
    idx = unstriped(offs)
    w2 = np.stack([unpack_weight(w2_words[e], w2_scales[e], "e2m1") for e in range(E)])
    w1 = np.stack([unpack_weight(w1_words[e], w1_scales[e], "e2m1") for e in range(E)])
    gq = mxq(f64(gate) * f64(dyT)[:, idx], 0, "e4m3")
    dh = by_expert(w2, gq)
    da = dh * d_relu2(f64(a))
    dx = by_expert(w1, mxq(da, 0, "e4m3"))
    return dx[:, unstriped(pos1)] + dx[:, unstriped(pos2)]

@@ -1,0 +1,201 @@
+from contextlib import ExitStack
+
+import concourse.mybir as mybir
+from concourse.masks import make_identity
+
+N, T, E, C, H, K = 1024, 768, 6, 256, 512, 512
+S = E * C
+FLOPS = 2 * S * (N * H + H * K)
+P = 128
+F32 = mybir.dt.float32
+BF16 = mybir.dt.bfloat16
+I32 = mybir.dt.int32
+U32 = mybir.dt.uint32
+U16 = mybir.dt.uint16
+U8 = mybir.dt.uint8
+FP8X4 = mybir.dt.float8_e4m3fn_x4
+FP4X4 = mybir.dt.float4_e2m1fn_x4
+MULT = mybir.AluOpType.mult
+ADD = mybir.AluOpType.add
+MAX = mybir.AluOpType.max
+COPY = mybir.ActivationFunctionType.Copy
+
+CHUNKS = [(0, 512),(512, 512),(1024, 256),(1280, 128),(1408, 128)]
+
+
+def tile_moe_bdx_mlp_relu2_kernel(tc, dyT, a, w2_words, w2_scales, w1_words, w1_scales, gate, offs, pos1, pos2, out):
+    nc = tc.nc
+    with ExitStack() as ctx:
+        lists = ctx.enter_context(tc.tile_pool(name="lists", bufs=1))
+        keep = ctx.enter_context(tc.tile_pool(name="keep", bufs=1))
+        stage = ctx.enter_context(tc.tile_pool(name="stage", bufs=3))
+        res = ctx.enter_context(tc.tile_pool(name="res", bufs=3))
+        ps_h = ctx.enter_context(tc.psum_pool(name="ps_h", bufs=2))
+        ps_t = ctx.enter_context(tc.psum_pool(name="ps_t", bufs=3))
+        ps_x = ctx.enter_context(tc.psum_pool(name="ps_x", bufs=3))
+
+        offs_sb = lists.tile([P, S // 16], U16, name="offs_sb")
+        pos1_sb = lists.tile([P, T // 16], U16, name="pos1_sb")
+        pos2_sb = lists.tile([P, T // 16], U16, name="pos2_sb")
+
+        ident = keep.tile([P, P], F32, name="ident")
+        s2 = keep.tile([P, 2 * E, H], U8, name="s2", align_bytes=64)
+        s1 = keep.tile([P, E, K], U8, name="s1", align_bytes=64)
+        w2 = [keep.tile([P, 2, 2 * H], U8, name=f"w2_{e}", align_bytes=64) for e in range(E)]
+        w1 = [keep.tile([P, 2 * K], U8, name=f"w1_{e}", align_bytes=64) for e in range(E)]
+        dy = [keep.tile([P, T], F32, name=f"dy_{m}") for m in range(8)]
+        gates = [keep.tile([P, 512], F32, name=f"gate_{b}") for b in range(3)]
+        acts = [keep.tile([P, 4, 512], F32, name=f"act_{b}") for b in range(3)]
+        dx = keep.tile([P, 4, S], F32, name="dx")
+
+        nc.gpsimd.memset(s2[:].rearrange("p g i -> p (g i)").bitcast(I32), 0)
+        nc.gpsimd.memset(s1[:].rearrange("p g i -> p (g i)").bitcast(I32), 0)
+        make_identity(nc, ident[:])
+
+        dy_src = dyT.rearrange("(s p j) t -> s j p t", s=2, j=4)
+        a_src = a.rearrange("(p t) c -> p t c", t=4)
+
+        def load_gate(b):
+            nc.sync.dma_start(out=gates[b][:], in_=gate[0:P, b * 512 : (b + 1) * 512])
+
+        def load_act(b):
+            nc.sync.dma_start(out=acts[b][:], in_=a_src[:, :, b * 512 : (b + 1) * 512])
+
+        def load_w(e):
+            nc.sync.dma_start(out=w2[e][:].bitcast(I32), in_=w2_words[e].rearrange("s p b -> p s b").bitcast(I32))
+            nc.sync.dma_start(out=w1[e][:].bitcast(I32), in_=w1_words[e, 0].bitcast(I32))
+
+        nc.sync.dma_start(offs_sb[:], offs)
+        load_gate(0)
+        for m in range(8):
+            nc.sync.dma_start(out=dy[m][:], in_=dy_src[m // 4, m % 4])
+        s2_src = w2_scales.bitcast(I32).rearrange("e s f i -> f (e s) i")
+        s1_src = w1_scales.bitcast(I32).rearrange("e s f i -> f (e s) i")
+        for q in range(4):
+            nc.sync.dma_start(out=s2[32 * q : 32 * q + 4].bitcast(I32), in_=s2_src[4 * q : 4 * q + 4])
+        for q in range(4):
+            nc.sync.dma_start(out=s1[32 * q : 32 * q + 4].bitcast(I32), in_=s1_src[4 * q : 4 * q + 4])
+        load_w(0)
+        load_w(1)
+        load_act(0)
+        load_gate(1)
+        load_w(2)
+        load_w(3)
+        load_act(1)
+        load_gate(2)
+        load_w(4)
+        load_w(5)
+        load_act(2)
+        nc.sync.dma_start(pos1_sb[:], pos1)
+        nc.sync.dma_start(pos2_sb[:], pos2)
+
+        codes = {}
+        da_in = {}
+
+        def gather(c, s):
+            c0, n = CHUNKS[c]
+            g = stage.tile([P, 4, n], F32, name="g")
+            for j in range(4):
+                nc.vector.tensor_tensor(
+                    g[:, j, :],
+                    dy[4 * s + j][:].indirect(offs_sb[:, c0 // 16 : (c0 + n) // 16]),
+                    gates[c0 // 512][:, c0 % 512 : c0 % 512 + n],
+                    MULT,
+                )
+            gb = stage.tile([P, n, 4], BF16, name="gb", align_bytes=64)
+            nc.scalar.copy(out=gb[:], in_=g[:].rearrange("p j c -> p c j"))
+            return gb
+
+        def quant(c, s, gb):
+            n = CHUNKS[c][1]
+            w = stage.tile([P, n], U32, name=f"gc{s}", align_bytes=64)
+            z = stage.tile([P, n], U8, name=f"gz{s}", align_bytes=64)
+            nc.vector.quantize_mx(out=w[:].bitcast(FP8X4), scales=z[:], in_=gb[:].rearrange("p c j -> p (c j)"))
+            codes[c, s] = (w, z)
+
+        def first(c):
+            c0, n = CHUNKS[c]
+            for b in range(n // P):
+                e = (c0 + b * P) // C
+                acc = ps_h.tile([P, H], F32, name="acc")
+                for s in range(2):
+                    w, z = codes[c, s]
+                    nc.tensor.matmul_mx(
+                        out=acc[:],
+                        lhsT=w[:, b * P : (b + 1) * P].bitcast(FP8X4),
+                        lhsT_scale=z[:, b * P : (b + 1) * P],
+                        rhs=w2[e][:, s, :].bitcast(FP4X4),
+                        rhs_scale=s2[:, 2 * e + s, :],
+                        start=(s == 0),
+                        stop=(s == 1),
+                    )
+                ht = stage.tile([P, 4, P], F32, name="ht")
+                nc.scalar.copy(out=ht[:], in_=acc[:].rearrange("p (m t) -> p t m", t=4))
+                tr = ps_t.tile([P, 4, P], F32, name="tr")
+                for t in range(4):
+                    nc.tensor.transpose(tr[:, t, :], ht[:, t, :], ident[:])
+                da_in[c, b] = tr
+
+        def second(c):
+            c0, n = CHUNKS[c]
+            for h0 in range(0, n, C):
+                width = min(C, n)
+                db = stage.tile([P, width, 4], BF16, name="db", align_bytes=64)
+                for b in range(width // P):
+                    col = c0 + h0 + b * P
+                    nc.vector.scalar_tensor_tensor(
+                        out=db[:, b * P : (b + 1) * P, :],
+                        in0=acts[col // 512][:, :, col % 512 : col % 512 + P].rearrange("p t c -> p c t"),
+                        scalar=0.0,
+                        in1=da_in[c, h0 // P + b][:].rearrange("p t c -> p c t"),
+                        op0=MAX,
+                        op1=MULT,
+                    )
+                w = stage.tile([P, width], U32, name="dc", align_bytes=64)
+                z = stage.tile([P, width], U8, name="dz", align_bytes=64)
+                nc.vector.quantize_mx(out=w[:].bitcast(FP8X4), scales=z[:], in_=db[:].rearrange("p c t -> p (c t)"))
+                e = (c0 + h0) // C
+                per = 512 // width
+                for k0 in range(0, 4, per):
+                    acc = ps_x.tile([P, per, width], F32, name="xacc")
+                    for k in range(per):
+                        cols = slice((k0 + k) * P, (k0 + k + 1) * P)
+                        nc.tensor.matmul_mx(
+                            out=acc[:, k, :],
+                            lhsT=w1[e][:, 2 * (k0 + k) * P : 2 * (k0 + k + 1) * P].bitcast(FP4X4),
+                            lhsT_scale=s1[:, e, cols],
+                            rhs=w[:].bitcast(FP8X4),
+                            rhs_scale=z[:],
+                            start=True,
+                            stop=True,
+                        )
+                    nc.scalar.activation(out=dx[:, k0 : k0 + per, c0 + h0 : c0 + h0 + width], in_=acc[:], func=COPY, scale=2.0)
+
+        pend = None
+        for c in range(len(CHUNKS)):
+            gb0 = gather(c, 0)
+            if pend is not None:
+                quant(c - 1, 1, pend)
+                first(c - 1)
+            gb1 = gather(c, 1)
+            quant(c, 0, gb0)
+            if pend is not None:
+                second(c - 1)
+            pend = gb1
+        last = len(CHUNKS) - 1
+        quant(last, 1, pend)
+        first(last)
+        second(last)
+
+        for k in range(4):
+            parts = 1 if k < 3 else 2
+            n = T // parts
+            for h in range(parts):
+                cols = slice(h * n // 16, (h + 1) * n // 16)
+                x1 = res.tile([P, n], F32, name="x1")
+                x2 = res.tile([P, n], F32, name="x2")
+                nc.vector.tensor_copy(x1[:], dx[:, k, :].indirect(pos1_sb[:, cols]))
+                nc.vector.tensor_copy(x2[:], dx[:, k, :].indirect(pos2_sb[:, cols]))
+                o = res.tile([P, n], F32, name="o")
+                nc.vector.tensor_tensor(o[:], x1[:], x2[:], ADD)
+                nc.sync.dma_start(out=out[k * P : (k + 1) * P, h * n : (h + 1) * n], in_=o[:])

@@ -5,8 +5,10 @@ from concourse.masks import make_identity
 
 N, T, E, C, H, K = 1024, 768, 6, 256, 512, 512
 S = E * C
-FLOPS = 2 * S * (N * H + H * K)
 P = 128
+PACK = 4
+FLOPS = 2 * S * (N * H + H * K)
+
 F32 = mybir.dt.float32
 BF16 = mybir.dt.bfloat16
 I32 = mybir.dt.int32
@@ -20,182 +22,213 @@ ADD = mybir.AluOpType.add
 MAX = mybir.AluOpType.max
 COPY = mybir.ActivationFunctionType.Copy
 
-CHUNKS = [(0, 512),(512, 512),(1024, 256),(1280, 128),(1408, 128)]
+CHUNKS = ((0, 512), (512, 384), (896, 384), (1280, 256))
 
 
-def tile_moe_bdx_mlp_relu2_kernel(tc, dyT, a, w2_words, w2_scales, w1_words, w1_scales, gate, offs, pos1, pos2, out):
+def tile_moe_bdx_mlp_relu2_kernel(
+    tc, dyT, a, w2_words, w2_scales, w1_words, w1_scales, gate, offs, pos1, pos2, out
+):
     nc = tc.nc
     with ExitStack() as ctx:
         lists = ctx.enter_context(tc.tile_pool(name="lists", bufs=1))
         keep = ctx.enter_context(tc.tile_pool(name="keep", bufs=1))
         stage = ctx.enter_context(tc.tile_pool(name="stage", bufs=3))
-        res = ctx.enter_context(tc.tile_pool(name="res", bufs=3))
-        ps_h = ctx.enter_context(tc.psum_pool(name="ps_h", bufs=2))
-        ps_t = ctx.enter_context(tc.psum_pool(name="ps_t", bufs=3))
-        ps_x = ctx.enter_context(tc.psum_pool(name="ps_x", bufs=3))
+        ps_dh = ctx.enter_context(tc.psum_pool(name="ps_dh", bufs=3))
+        ps_turn = ctx.enter_context(tc.psum_pool(name="ps_turn", bufs=3))
+        ps_dx = ctx.enter_context(tc.psum_pool(name="ps_dx", bufs=2))
 
         offs_sb = lists.tile([P, S // 16], U16, name="offs_sb")
         pos1_sb = lists.tile([P, T // 16], U16, name="pos1_sb")
         pos2_sb = lists.tile([P, T // 16], U16, name="pos2_sb")
 
         ident = keep.tile([P, P], F32, name="ident")
-        s2 = keep.tile([P, 2 * E, H], U8, name="s2", align_bytes=64)
-        s1 = keep.tile([P, E, K], U8, name="s1", align_bytes=64)
+        w2_sc = keep.tile([P, 2 * E, H], U8, name="w2_sc", align_bytes=64)
+        w1_sc = keep.tile([P, E, K], U8, name="w1_sc", align_bytes=64)
         w2 = [keep.tile([P, 2, 2 * H], U8, name=f"w2_{e}", align_bytes=64) for e in range(E)]
         w1 = [keep.tile([P, 2 * K], U8, name=f"w1_{e}", align_bytes=64) for e in range(E)]
-        dy = [keep.tile([P, T], F32, name=f"dy_{m}") for m in range(8)]
-        gates = [keep.tile([P, 512], F32, name=f"gate_{b}") for b in range(3)]
-        acts = [keep.tile([P, 4, 512], F32, name=f"act_{b}") for b in range(3)]
-        dx = keep.tile([P, 4, S], F32, name="dx")
+        dy = [keep.tile([P, T], F32, name=f"dy_{m}") for m in range(N // P)]
+        gates = [keep.tile([P, n], F32, name=f"gate_{c0}") for c0, n in CHUNKS]
+        saved = [keep.tile([P, PACK, 2 * C], F32, name=f"saved_{b}") for b in range(3)]
+        da_codes = [keep.tile([P, C], U32, name=f"da_codes_{e}", align_bytes=64) for e in range(E)]
+        da_scales = [keep.tile([P, C], U8, name=f"da_scales_{e}", align_bytes=64) for e in range(E)]
+        dx = keep.tile([P, K // P, S], F32, name="dx")
 
-        nc.gpsimd.memset(s2[:].rearrange("p g i -> p (g i)").bitcast(I32), 0)
-        nc.gpsimd.memset(s1[:].rearrange("p g i -> p (g i)").bitcast(I32), 0)
+        nc.gpsimd.memset(w2_sc[:].rearrange("p g i -> p (g i)").bitcast(I32), 0)
+        nc.gpsimd.memset(w1_sc[:].rearrange("p g i -> p (g i)").bitcast(I32), 0)
         make_identity(nc, ident[:])
 
-        dy_src = dyT.rearrange("(s p j) t -> s j p t", s=2, j=4)
-        a_src = a.rearrange("(p t) c -> p t c", t=4)
+        dy_rows = dyT.rearrange("(s p j) t -> s j p t", s=2, j=PACK)
+        a_rows = a.rearrange("(p t) c -> p t c", t=PACK)
+        w2_rows = w2_scales.bitcast(I32).rearrange("e s f i -> f (e s) i")
+        w1_rows = w1_scales.bitcast(I32).rearrange("e s f i -> f (e s) i")
 
-        def load_gate(b):
-            nc.sync.dma_start(out=gates[b][:], in_=gate[0:P, b * 512 : (b + 1) * 512])
+        def load_gate(c):
+            c0, n = CHUNKS[c]
+            nc.sync.dma_start(out=gates[c][:], in_=gate[0:P, c0 : c0 + n])
 
-        def load_act(b):
-            nc.sync.dma_start(out=acts[b][:], in_=a_src[:, :, b * 512 : (b + 1) * 512])
+        def load_saved(b):
+            nc.sync.dma_start(out=saved[b][:], in_=a_rows[:, :, 2 * C * b : 2 * C * (b + 1)])
 
-        def load_w(e):
+        def load_w2(e):
             nc.sync.dma_start(out=w2[e][:].bitcast(I32), in_=w2_words[e].rearrange("s p b -> p s b").bitcast(I32))
+
+        def load_w1(e):
             nc.sync.dma_start(out=w1[e][:].bitcast(I32), in_=w1_words[e, 0].bitcast(I32))
 
         nc.sync.dma_start(offs_sb[:], offs)
         load_gate(0)
-        for m in range(8):
-            nc.sync.dma_start(out=dy[m][:], in_=dy_src[m // 4, m % 4])
-        s2_src = w2_scales.bitcast(I32).rearrange("e s f i -> f (e s) i")
-        s1_src = w1_scales.bitcast(I32).rearrange("e s f i -> f (e s) i")
-        for q in range(4):
-            nc.sync.dma_start(out=s2[32 * q : 32 * q + 4].bitcast(I32), in_=s2_src[4 * q : 4 * q + 4])
-        for q in range(4):
-            nc.sync.dma_start(out=s1[32 * q : 32 * q + 4].bitcast(I32), in_=s1_src[4 * q : 4 * q + 4])
-        load_w(0)
-        load_w(1)
-        load_act(0)
+        for m in range(N // P):
+            nc.sync.dma_start(out=dy[m][:], in_=dy_rows[m // PACK, m % PACK])
         load_gate(1)
-        load_w(2)
-        load_w(3)
-        load_act(1)
-        load_gate(2)
-        load_w(4)
-        load_w(5)
-        load_act(2)
+        for q in range(4):
+            nc.sync.dma_start(out=w2_sc[32 * q : 32 * q + 4].bitcast(I32), in_=w2_rows[4 * q : 4 * q + 4])
+        for q in range(4):
+            nc.sync.dma_start(out=w1_sc[32 * q : 32 * q + 4].bitcast(I32), in_=w1_rows[4 * q : 4 * q + 4])
+        for e in range(E):
+            load_w2(e)
+        for c in range(2, len(CHUNKS)):
+            load_gate(c)
+        load_saved(0)
+        load_w1(0)
         nc.sync.dma_start(pos1_sb[:], pos1)
         nc.sync.dma_start(pos2_sb[:], pos2)
+        for b in range(1, 3):
+            load_saved(b)
+        for e in range(1, E):
+            load_w1(e)
 
-        codes = {}
-        da_in = {}
+        rounded = {}
+        g_codes = {}
+        turned = {}
 
-        def gather(c, s):
+        def gather(c, s, meanwhile):
             c0, n = CHUNKS[c]
-            g = stage.tile([P, 4, n], F32, name="g")
-            for j in range(4):
+            g = stage.tile([P, PACK, n], F32, name="g")
+            for j in range(PACK):
+                if j == PACK - 1:
+                    meanwhile()
                 nc.vector.tensor_tensor(
-                    g[:, j, :],
-                    dy[4 * s + j][:].indirect(offs_sb[:, c0 // 16 : (c0 + n) // 16]),
-                    gates[c0 // 512][:, c0 % 512 : c0 % 512 + n],
-                    MULT,
+                    g[:, j, :], dy[PACK * s + j][:].indirect(offs_sb[:, c0 // 16 : (c0 + n) // 16]), gates[c][:], MULT
                 )
-            gb = stage.tile([P, n, 4], BF16, name="gb", align_bytes=64)
-            nc.scalar.copy(out=gb[:], in_=g[:].rearrange("p j c -> p c j"))
-            return gb
+            rounded[c, s] = stage.tile([P, n, PACK], BF16, name="g_bf16", align_bytes=64)
+            nc.scalar.copy(out=rounded[c, s][:], in_=g[:].rearrange("p j c -> p c j"))
 
-        def quant(c, s, gb):
-            n = CHUNKS[c][1]
-            w = stage.tile([P, n], U32, name=f"gc{s}", align_bytes=64)
-            z = stage.tile([P, n], U8, name=f"gz{s}", align_bytes=64)
-            nc.vector.quantize_mx(out=w[:].bitcast(FP8X4), scales=z[:], in_=gb[:].rearrange("p c j -> p (c j)"))
-            codes[c, s] = (w, z)
-
-        def first(c):
+        def quantise(c, s):
             c0, n = CHUNKS[c]
+            codes = stage.tile([P, n], U32, name=f"g_codes_{s}", align_bytes=64)
+            scales = stage.tile([P, n], U8, name=f"g_scales_{s}", align_bytes=64)
+            flat = rounded[c, s][:].rearrange("p c j -> p (c j)")
+            done = 0
+            for width in (512, 256, 128):
+                if n - done >= width:
+                    cols = slice(done, done + width)
+                    nc.vector.quantize_mx(
+                        out=codes[:, cols].bitcast(FP8X4),
+                        scales=scales[:, cols],
+                        in_=flat[:, PACK * done : PACK * (done + width)],
+                    )
+                    done += width
             for b in range(n // P):
-                e = (c0 + b * P) // C
-                acc = ps_h.tile([P, H], F32, name="acc")
-                for s in range(2):
-                    w, z = codes[c, s]
-                    nc.tensor.matmul_mx(
-                        out=acc[:],
-                        lhsT=w[:, b * P : (b + 1) * P].bitcast(FP8X4),
-                        lhsT_scale=z[:, b * P : (b + 1) * P],
-                        rhs=w2[e][:, s, :].bitcast(FP4X4),
-                        rhs_scale=s2[:, 2 * e + s, :],
-                        start=(s == 0),
-                        stop=(s == 1),
-                    )
-                ht = stage.tile([P, 4, P], F32, name="ht")
-                nc.scalar.copy(out=ht[:], in_=acc[:].rearrange("p (m t) -> p t m", t=4))
-                tr = ps_t.tile([P, 4, P], F32, name="tr")
-                for t in range(4):
-                    nc.tensor.transpose(tr[:, t, :], ht[:, t, :], ident[:])
-                da_in[c, b] = tr
+                cols = slice(b * P, (b + 1) * P)
+                g_codes[c0 // P + b, s] = (codes[:, cols], scales[:, cols])
 
-        def second(c):
+        def product_dh(b):
+            e = b * P // C
+            acc = ps_dh.tile([P, H], F32, name="dh")
+            for s in range(2):
+                codes, scales = g_codes[b, s]
+                nc.tensor.matmul_mx(
+                    out=acc[:],
+                    lhsT=codes.bitcast(FP8X4),
+                    lhsT_scale=scales,
+                    rhs=w2[e][:, s, :].bitcast(FP4X4),
+                    rhs_scale=w2_sc[:, 2 * e + s, :],
+                    start=(s == 0),
+                    stop=(s == 1),
+                )
+            dh = stage.tile([P, PACK, P], F32, name="dh_sb")
+            nc.scalar.copy(out=dh[:], in_=acc[:].rearrange("p (m t) -> p t m", t=PACK))
+            return dh
+
+        def turn(b, dh):
+            turned[b] = ps_turn.tile([P, PACK, P], F32, name="turned")
+            for t in range(PACK):
+                nc.tensor.transpose(turned[b][:, t, :], dh[:, t, :], ident[:])
+
+        def first_layer(c):
+            quantise(c, 1)
             c0, n = CHUNKS[c]
-            for h0 in range(0, n, C):
-                width = min(C, n)
-                db = stage.tile([P, width, 4], BF16, name="db", align_bytes=64)
-                for b in range(width // P):
-                    col = c0 + h0 + b * P
-                    nc.vector.scalar_tensor_tensor(
-                        out=db[:, b * P : (b + 1) * P, :],
-                        in0=acts[col // 512][:, :, col % 512 : col % 512 + P].rearrange("p t c -> p c t"),
-                        scalar=0.0,
-                        in1=da_in[c, h0 // P + b][:].rearrange("p t c -> p c t"),
-                        op0=MAX,
-                        op1=MULT,
-                    )
-                w = stage.tile([P, width], U32, name="dc", align_bytes=64)
-                z = stage.tile([P, width], U8, name="dz", align_bytes=64)
-                nc.vector.quantize_mx(out=w[:].bitcast(FP8X4), scales=z[:], in_=db[:].rearrange("p c t -> p (c t)"))
-                e = (c0 + h0) // C
-                per = 512 // width
-                for k0 in range(0, 4, per):
-                    acc = ps_x.tile([P, per, width], F32, name="xacc")
-                    for k in range(per):
-                        cols = slice((k0 + k) * P, (k0 + k + 1) * P)
-                        nc.tensor.matmul_mx(
-                            out=acc[:, k, :],
-                            lhsT=w1[e][:, 2 * (k0 + k) * P : 2 * (k0 + k + 1) * P].bitcast(FP4X4),
-                            lhsT_scale=s1[:, e, cols],
-                            rhs=w[:].bitcast(FP8X4),
-                            rhs_scale=z[:],
-                            start=True,
-                            stop=True,
-                        )
-                    nc.scalar.activation(out=dx[:, k0 : k0 + per, c0 + h0 : c0 + h0 + width], in_=acc[:], func=COPY, scale=2.0)
+            blocks = range(c0 // P, (c0 + n) // P)
+            dh = product_dh(blocks[0])
+            for b in blocks[1:]:
+                following = product_dh(b)
+                turn(b - 1, dh)
+                dh = following
+            turn(blocks[-1], dh)
 
-        pend = None
-        for c in range(len(CHUNKS)):
-            gb0 = gather(c, 0)
-            if pend is not None:
-                quant(c - 1, 1, pend)
-                first(c - 1)
-            gb1 = gather(c, 1)
-            quant(c, 0, gb0)
-            if pend is not None:
-                second(c - 1)
-            pend = gb1
+        def make_da(e):
+            da = stage.tile([P, C, PACK], BF16, name="da", align_bytes=64)
+            for h in range(C // P):
+                b = e * C // P + h
+                cols = slice(b * P % (2 * C), b * P % (2 * C) + P)
+                nc.vector.scalar_tensor_tensor(
+                    out=da[:, h * P : (h + 1) * P, :],
+                    in0=saved[b * P // (2 * C)][:, :, cols].rearrange("p t c -> p c t"),
+                    scalar=0.0,
+                    in1=turned[b][:].rearrange("p t c -> p c t"),
+                    op0=MAX,
+                    op1=MULT,
+                )
+            nc.vector.quantize_mx(
+                out=da_codes[e][:].bitcast(FP8X4), scales=da_scales[e][:], in_=da[:].rearrange("p c t -> p (c t)")
+            )
+
+        def product_dx(e, k0, k1, on_vector=False):
+            acc = ps_dx.tile([P, k1 - k0, C], F32, name="dx_acc")
+            for k in range(k0, k1):
+                nc.tensor.matmul_mx(
+                    out=acc[:, k - k0, :],
+                    lhsT=w1[e][:, 2 * k * P : 2 * (k + 1) * P].bitcast(FP4X4),
+                    lhsT_scale=w1_sc[:, e, k * P : (k + 1) * P],
+                    rhs=da_codes[e][:].bitcast(FP8X4),
+                    rhs_scale=da_scales[e][:],
+                    start=True,
+                    stop=True,
+                )
+            slots = dx[:, k0:k1, e * C : (e + 1) * C]
+            if on_vector:
+                nc.vector.tensor_scalar(slots, acc[:], 2.0, None, MULT)
+            else:
+                nc.scalar.activation(out=slots, in_=acc[:], func=COPY, scale=2.0)
+
+        def expert_0():
+            quantise(last, 0)
+            make_da(0)
+            product_dx(0, 0, 2)
+            product_dx(0, 2, 4)
+
         last = len(CHUNKS) - 1
-        quant(last, 1, pend)
-        first(last)
-        second(last)
+        for c in range(last + 1):
+            gather(c, 0, (lambda: first_layer(c - 1)) if c else (lambda: None))
+            gather(c, 1, (lambda: quantise(c, 0)) if c < last else expert_0)
+        first_layer(last)
+        for e in range(1, E):
+            make_da(e)
+            if e < E - 1:
+                product_dx(e, 0, 2)
+            else:
+                product_dx(e, 0, 1, on_vector=True)
+                product_dx(e, 1, 2)
+        for e in range(1, E):
+            product_dx(e, 2, 4)
 
-        for k in range(4):
-            parts = 1 if k < 3 else 2
-            n = T // parts
-            for h in range(parts):
-                cols = slice(h * n // 16, (h + 1) * n // 16)
-                x1 = res.tile([P, n], F32, name="x1")
-                x2 = res.tile([P, n], F32, name="x2")
-                nc.vector.tensor_copy(x1[:], dx[:, k, :].indirect(pos1_sb[:, cols]))
-                nc.vector.tensor_copy(x2[:], dx[:, k, :].indirect(pos2_sb[:, cols]))
-                o = res.tile([P, n], F32, name="o")
-                nc.vector.tensor_tensor(o[:], x1[:], x2[:], ADD)
-                nc.sync.dma_start(out=out[k * P : (k + 1) * P, h * n : (h + 1) * n], in_=o[:])
+        for k in range(K // P):
+            x1 = stage.tile([P, T], F32, name="x1")
+            x2 = stage.tile([P, T], F32, name="x2")
+            total = stage.tile([P, T], F32, name="total")
+            nc.vector.tensor_copy(x1[:], dx[:, k, :].indirect(pos1_sb[:]))
+            for c0, c1 in ((0, T),) if k < K // P - 1 else ((0, T // 2), (T // 2, T)):
+                nc.vector.tensor_copy(x2[:, c0:c1], dx[:, k, :].indirect(pos2_sb[:, c0 // 16 : c1 // 16]))
+                adder = nc.vector if c0 else nc.gpsimd
+                adder.tensor_tensor(total[:, c0:c1], x1[:, c0:c1], x2[:, c0:c1], ADD)
+                nc.sync.dma_start(out=out[k * P : (k + 1) * P, c0:c1], in_=total[:, c0:c1])

@@ -20,9 +20,11 @@ FP4X4 = mybir.dt.float4_e2m1fn_x4
 MULT = mybir.AluOpType.mult
 ADD = mybir.AluOpType.add
 MAX = mybir.AluOpType.max
+RELU = mybir.ActivationFunctionType.Relu
 COPY = mybir.ActivationFunctionType.Copy
 
-CHUNKS = ((0, 512), (512, 384), (896, 384), (1280, 256))
+CHUNKS = ((0, 384), (384, 384), (768, 384), (1152, 256), (1408, 128))
+ON_GPSIMD = (0, 1)
 
 
 def tile_moe_bdx_mlp_relu2_kernel(
@@ -34,8 +36,8 @@ def tile_moe_bdx_mlp_relu2_kernel(
         keep = ctx.enter_context(tc.tile_pool(name="keep", bufs=1))
         stage = ctx.enter_context(tc.tile_pool(name="stage", bufs=3))
         ps_dh = ctx.enter_context(tc.psum_pool(name="ps_dh", bufs=3))
-        ps_turn = ctx.enter_context(tc.psum_pool(name="ps_turn", bufs=3))
-        ps_dx = ctx.enter_context(tc.psum_pool(name="ps_dx", bufs=2))
+        ps_turn = ctx.enter_context(tc.psum_pool(name="ps_turn", bufs=2))
+        ps_dx = ctx.enter_context(tc.psum_pool(name="ps_dx", bufs=3))
 
         offs_sb = lists.tile([P, S // 16], U16, name="offs_sb")
         pos1_sb = lists.tile([P, T // 16], U16, name="pos1_sb")
@@ -51,6 +53,8 @@ def tile_moe_bdx_mlp_relu2_kernel(
         saved = [keep.tile([P, PACK, 2 * C], F32, name=f"saved_{b}") for b in range(3)]
         da_codes = [keep.tile([P, C], U32, name=f"da_codes_{e}", align_bytes=64) for e in range(E)]
         da_scales = [keep.tile([P, C], U8, name=f"da_scales_{e}", align_bytes=64) for e in range(E)]
+        relu_a = [keep.tile([P, C, PACK], F32, name=f"relu_a_{e}") for e in ON_GPSIMD]
+        dh_copy = [keep.tile([P, C, PACK], F32, name=f"dh_copy_{e}") for e in ON_GPSIMD]
         dx = keep.tile([P, K // P, S], F32, name="dx")
 
         nc.gpsimd.memset(w2_sc[:].rearrange("p g i -> p (g i)").bitcast(I32), 0)
@@ -100,18 +104,21 @@ def tile_moe_bdx_mlp_relu2_kernel(
         rounded = {}
         g_codes = {}
         turned = {}
+        products = {}
 
-        def gather(c, s, meanwhile):
+        def gather(c, s, meanwhile=None):
             c0, n = CHUNKS[c]
-            g = stage.tile([P, PACK, n], F32, name="g")
+            g = stage.tile([P, PACK, n], F32, name="g", align_bytes=64)
             for j in range(PACK):
-                if j == PACK - 1:
+                if j == PACK - 1 and meanwhile:
                     meanwhile()
                 nc.vector.tensor_tensor(
                     g[:, j, :], dy[PACK * s + j][:].indirect(offs_sb[:, c0 // 16 : (c0 + n) // 16]), gates[c][:], MULT
                 )
             rounded[c, s] = stage.tile([P, n, PACK], BF16, name="g_bf16", align_bytes=64)
-            nc.scalar.copy(out=rounded[c, s][:], in_=g[:].rearrange("p j c -> p c j"))
+            nc.scalar.copy(
+                out=rounded[c, s][:].rearrange("p (c i) j -> p c j i", i=4), in_=g[:].rearrange("p j (c i) -> p c j i", i=4)
+            )
 
         def quantise(c, s):
             c0, n = CHUNKS[c]
@@ -165,23 +172,33 @@ def tile_moe_bdx_mlp_relu2_kernel(
                 turn(b - 1, dh)
                 dh = following
             turn(blocks[-1], dh)
+            for b in blocks:
+                e, h = divmod(b, C // P)
+                if e in ON_GPSIMD:
+                    nc.scalar.copy(
+                        out=dh_copy[e][:, h * P : (h + 1) * P, :], in_=turned[b][:].rearrange("p t c -> p c t")
+                    )
+
+        def slots_of(b):
+            cols = slice(b * P % (2 * C), b * P % (2 * C) + P)
+            return saved[b * P // (2 * C)][:, :, cols].rearrange("p t c -> p c t")
 
         def make_da(e):
-            da = stage.tile([P, C, PACK], BF16, name="da", align_bytes=64)
+            da = stage.tile([P, C, PACK], BF16, name="g" if e == len(ON_GPSIMD) else "da", align_bytes=64)
             for h in range(C // P):
                 b = e * C // P + h
-                cols = slice(b * P % (2 * C), b * P % (2 * C) + P)
                 nc.vector.scalar_tensor_tensor(
                     out=da[:, h * P : (h + 1) * P, :],
-                    in0=saved[b * P // (2 * C)][:, :, cols].rearrange("p t c -> p c t"),
+                    in0=slots_of(b),
                     scalar=0.0,
                     in1=turned[b][:].rearrange("p t c -> p c t"),
                     op0=MAX,
                     op1=MULT,
                 )
-            nc.vector.quantize_mx(
-                out=da_codes[e][:].bitcast(FP8X4), scales=da_scales[e][:], in_=da[:].rearrange("p c t -> p (c t)")
-            )
+            products[e] = da[:].rearrange("p c t -> p (c t)")
+
+        def quantise_da(e):
+            nc.vector.quantize_mx(out=da_codes[e][:].bitcast(FP8X4), scales=da_scales[e][:], in_=products[e])
 
         def product_dx(e, k0, k1, on_vector=False):
             acc = ps_dx.tile([P, k1 - k0, C], F32, name="dx_acc")
@@ -201,25 +218,36 @@ def tile_moe_bdx_mlp_relu2_kernel(
             else:
                 nc.scalar.activation(out=slots, in_=acc[:], func=COPY, scale=2.0)
 
-        def expert_0():
-            quantise(last, 0)
-            make_da(0)
-            product_dx(0, 0, 2)
-            product_dx(0, 2, 4)
-
         last = len(CHUNKS) - 1
         for c in range(last + 1):
-            gather(c, 0, (lambda: first_layer(c - 1)) if c else (lambda: None))
-            gather(c, 1, (lambda: quantise(c, 0)) if c < last else expert_0)
+            gather(c, 0)
+            if c:
+                first_layer(c - 1)
+            if c == 1:
+                for e in ON_GPSIMD:
+                    for h in range(C // P):
+                        nc.scalar.activation(
+                            out=relu_a[e][:, h * P : (h + 1) * P, :], in_=slots_of(e * C // P + h), func=RELU
+                        )
+            gather(c, 1, lambda: quantise(c, 0))
+        make_da(2)
+        shared = stage.tile([P, len(ON_GPSIMD), C, PACK], BF16, name="g", align_bytes=64)
+        for e in ON_GPSIMD:
+            for h in range(C // P):
+                part = slice(h * P, (h + 1) * P)
+                nc.gpsimd.tensor_tensor(shared[:, e, part, :], dh_copy[e][:, part, :], relu_a[e][:, part, :], MULT)
+            products[e] = shared[:, e, :, :].rearrange("p c t -> p (c t)")
         first_layer(last)
-        for e in range(1, E):
-            make_da(e)
+        for e in (2, 0, 3, 1, 4, 5):
+            if e > 2:
+                make_da(e)
+            quantise_da(e)
             if e < E - 1:
                 product_dx(e, 0, 2)
             else:
                 product_dx(e, 0, 1, on_vector=True)
                 product_dx(e, 1, 2)
-        for e in range(1, E):
+        for e in (2, 0, 3, 1, 4, 5):
             product_dx(e, 2, 4)
 
         for k in range(K // P):

@@ -86,20 +86,24 @@ def tile_moe_bdx_mlp_relu2_kernel(
         load_gate(1)
         for q in range(4):
             nc.sync.dma_start(out=w2_sc[32 * q : 32 * q + 4].bitcast(I32), in_=w2_rows[4 * q : 4 * q + 4])
+        load_w2(0)
+        load_w2(1)
+        load_saved(0)
+        load_gate(2)
+        load_w2(2)
+        load_w2(3)
+        load_gate(3)
+        load_gate(4)
+        load_w2(4)
+        load_w2(5)
+        load_saved(1)
         for q in range(4):
             nc.sync.dma_start(out=w1_sc[32 * q : 32 * q + 4].bitcast(I32), in_=w1_rows[4 * q : 4 * q + 4])
+        load_saved(2)
         for e in range(E):
-            load_w2(e)
-        for c in range(2, len(CHUNKS)):
-            load_gate(c)
-        load_saved(0)
-        load_w1(0)
+            load_w1(e)
         nc.sync.dma_start(pos1_sb[:], pos1)
         nc.sync.dma_start(pos2_sb[:], pos2)
-        for b in range(1, 3):
-            load_saved(b)
-        for e in range(1, E):
-            load_w1(e)
 
         rounded = {}
         g_codes = {}
@@ -183,6 +187,13 @@ def tile_moe_bdx_mlp_relu2_kernel(
             cols = slice(b * P % (2 * C), b * P % (2 * C) + P)
             return saved[b * P // (2 * C)][:, :, cols].rearrange("p t c -> p c t")
 
+        def make_relu(e):
+            nc.scalar.activation(
+                out=relu_a[e][:].rearrange("p (c i) t -> p c t i", i=4),
+                in_=saved[0][:, :, e * C : (e + 1) * C].rearrange("p t (c i) -> p c t i", i=4),
+                func=RELU,
+            )
+
         def make_da(e):
             da = stage.tile([P, C, PACK], BF16, name="g" if e == len(ON_GPSIMD) else "da", align_bytes=64)
             for h in range(C // P):
@@ -225,10 +236,7 @@ def tile_moe_bdx_mlp_relu2_kernel(
                 first_layer(c - 1)
             if c == 1:
                 for e in ON_GPSIMD:
-                    for h in range(C // P):
-                        nc.scalar.activation(
-                            out=relu_a[e][:, h * P : (h + 1) * P, :], in_=slots_of(e * C // P + h), func=RELU
-                        )
+                    make_relu(e)
             gather(c, 1, lambda: quantise(c, 0))
         make_da(2)
         shared = stage.tile([P, len(ON_GPSIMD), C, PACK], BF16, name="g", align_bytes=64)

from contextlib import ExitStack

import concourse.mybir as mybir
from concourse.masks import make_identity

N, T, E, C, H, K = 1024, 768, 6, 256, 512, 512
S = E * C
P = 128
PACK = 4
FLOPS = 2 * S * (N * H + H * K)

F32 = mybir.dt.float32
BF16 = mybir.dt.bfloat16
I32 = mybir.dt.int32
U32 = mybir.dt.uint32
U16 = mybir.dt.uint16
U8 = mybir.dt.uint8
FP8X4 = mybir.dt.float8_e4m3fn_x4
FP4X4 = mybir.dt.float4_e2m1fn_x4
MULT = mybir.AluOpType.mult
ADD = mybir.AluOpType.add
MAX = mybir.AluOpType.max
RELU = mybir.ActivationFunctionType.Relu
COPY = mybir.ActivationFunctionType.Copy

CHUNKS = ((0, 384), (384, 384), (768, 384), (1152, 256), (1408, 128))
ON_GPSIMD = (0, 1)


def tile_moe_bdx_mlp_relu2_kernel(
    tc, dyT, a, w2_words, w2_scales, w1_words, w1_scales, gate, offs, pos1, pos2, out
):
    nc = tc.nc
    with ExitStack() as ctx:
        lists = ctx.enter_context(tc.tile_pool(name="lists", bufs=1))
        keep = ctx.enter_context(tc.tile_pool(name="keep", bufs=1))
        stage = ctx.enter_context(tc.tile_pool(name="stage", bufs=3))
        ps_dh = ctx.enter_context(tc.psum_pool(name="ps_dh", bufs=3))
        ps_turn = ctx.enter_context(tc.psum_pool(name="ps_turn", bufs=2))
        ps_dx = ctx.enter_context(tc.psum_pool(name="ps_dx", bufs=3))

        offs_sb = lists.tile([P, S // 16], U16, name="offs_sb")
        pos1_sb = lists.tile([P, T // 16], U16, name="pos1_sb")
        pos2_sb = lists.tile([P, T // 16], U16, name="pos2_sb")

        ident = keep.tile([P, P], F32, name="ident")
        w2_sc = keep.tile([P, 2 * E, H], U8, name="w2_sc", align_bytes=64)
        w1_sc = keep.tile([P, E, K], U8, name="w1_sc", align_bytes=64)
        w2 = [keep.tile([P, 2, 2 * H], U8, name=f"w2_{e}", align_bytes=64) for e in range(E)]
        w1 = [keep.tile([P, 2 * K], U8, name=f"w1_{e}", align_bytes=64) for e in range(E)]
        dy = [keep.tile([P, T], F32, name=f"dy_{m}") for m in range(N // P)]
        gates = [keep.tile([P, n], F32, name=f"gate_{c0}") for c0, n in CHUNKS]
        saved = [keep.tile([P, PACK, 2 * C], F32, name=f"saved_{b}") for b in range(3)]
        da_codes = [keep.tile([P, C], U32, name=f"da_codes_{e}", align_bytes=64) for e in range(E)]
        da_scales = [keep.tile([P, C], U8, name=f"da_scales_{e}", align_bytes=64) for e in range(E)]
        relu_a = [keep.tile([P, C, PACK], F32, name=f"relu_a_{e}") for e in ON_GPSIMD]
        dh_copy = [keep.tile([P, C, PACK], F32, name=f"dh_copy_{e}") for e in ON_GPSIMD]
        dx = keep.tile([P, K // P, S], F32, name="dx")

        nc.gpsimd.memset(w2_sc[:].rearrange("p g i -> p (g i)").bitcast(I32), 0)
        nc.gpsimd.memset(w1_sc[:].rearrange("p g i -> p (g i)").bitcast(I32), 0)
        make_identity(nc, ident[:])

        dy_rows = dyT.rearrange("(s p j) t -> s j p t", s=2, j=PACK)
        a_rows = a.rearrange("(p t) c -> p t c", t=PACK)
        w2_rows = w2_scales.bitcast(I32).rearrange("e s f i -> f (e s) i")
        w1_rows = w1_scales.bitcast(I32).rearrange("e s f i -> f (e s) i")

        def load_gate(c):
            c0, n = CHUNKS[c]
            nc.sync.dma_start(out=gates[c][:], in_=gate[0:P, c0 : c0 + n])

        def load_saved(b):
            nc.sync.dma_start(out=saved[b][:], in_=a_rows[:, :, 2 * C * b : 2 * C * (b + 1)])

        def load_w2(e):
            nc.sync.dma_start(out=w2[e][:].bitcast(I32), in_=w2_words[e].rearrange("s p b -> p s b").bitcast(I32))

        def load_w1(e):
            nc.sync.dma_start(out=w1[e][:].bitcast(I32), in_=w1_words[e, 0].bitcast(I32))

        nc.sync.dma_start(offs_sb[:], offs)
        load_gate(0)
        for m in range(N // P):
            nc.sync.dma_start(out=dy[m][:], in_=dy_rows[m // PACK, m % PACK])
        load_gate(1)
        for q in range(4):
            nc.sync.dma_start(out=w2_sc[32 * q : 32 * q + 4].bitcast(I32), in_=w2_rows[4 * q : 4 * q + 4])
        load_w2(0)
        load_w2(1)
        load_saved(0)
        load_gate(2)
        load_w2(2)
        load_w2(3)
        load_gate(3)
        load_gate(4)
        load_w2(4)
        load_w2(5)
        load_saved(1)
        for q in range(4):
            nc.sync.dma_start(out=w1_sc[32 * q : 32 * q + 4].bitcast(I32), in_=w1_rows[4 * q : 4 * q + 4])
        load_saved(2)
        for e in range(E):
            load_w1(e)
        nc.sync.dma_start(pos1_sb[:], pos1)
        nc.sync.dma_start(pos2_sb[:], pos2)

        rounded = {}
        g_codes = {}
        turned = {}
        products = {}

        def gather(c, s, meanwhile=None):
            c0, n = CHUNKS[c]
            g = stage.tile([P, PACK, n], F32, name="g", align_bytes=64)
            for j in range(PACK):
                if j == PACK - 1 and meanwhile:
                    meanwhile()
                nc.vector.tensor_tensor(
                    g[:, j, :], dy[PACK * s + j][:].indirect(offs_sb[:, c0 // 16 : (c0 + n) // 16]), gates[c][:], MULT
                )
            rounded[c, s] = stage.tile([P, n, PACK], BF16, name="g_bf16", align_bytes=64)
            nc.scalar.copy(
                out=rounded[c, s][:].rearrange("p (c i) j -> p c j i", i=4), in_=g[:].rearrange("p j (c i) -> p c j i", i=4)
            )

        def quantise(c, s):
            c0, n = CHUNKS[c]
            codes = stage.tile([P, n], U32, name=f"g_codes_{s}", align_bytes=64)
            scales = stage.tile([P, n], U8, name=f"g_scales_{s}", align_bytes=64)
            flat = rounded[c, s][:].rearrange("p c j -> p (c j)")
            done = 0
            for width in (512, 256, 128):
                if n - done >= width:
                    cols = slice(done, done + width)
                    nc.vector.quantize_mx(
                        out=codes[:, cols].bitcast(FP8X4),
                        scales=scales[:, cols],
                        in_=flat[:, PACK * done : PACK * (done + width)],
                    )
                    done += width
            for b in range(n // P):
                cols = slice(b * P, (b + 1) * P)
                g_codes[c0 // P + b, s] = (codes[:, cols], scales[:, cols])

        def product_dh(b):
            e = b * P // C
            acc = ps_dh.tile([P, H], F32, name="dh")
            for s in range(2):
                codes, scales = g_codes[b, s]
                nc.tensor.matmul_mx(
                    out=acc[:],
                    lhsT=codes.bitcast(FP8X4),
                    lhsT_scale=scales,
                    rhs=w2[e][:, s, :].bitcast(FP4X4),
                    rhs_scale=w2_sc[:, 2 * e + s, :],
                    start=(s == 0),
                    stop=(s == 1),
                )
            dh = stage.tile([P, PACK, P], F32, name="dh_sb")
            nc.scalar.copy(out=dh[:], in_=acc[:].rearrange("p (m t) -> p t m", t=PACK))
            return dh

        def turn(b, dh):
            turned[b] = ps_turn.tile([P, PACK, P], F32, name="turned")
            for t in range(PACK):
                nc.tensor.transpose(turned[b][:, t, :], dh[:, t, :], ident[:])

        def first_layer(c):
            quantise(c, 1)
            c0, n = CHUNKS[c]
            blocks = range(c0 // P, (c0 + n) // P)
            dh = product_dh(blocks[0])
            for b in blocks[1:]:
                following = product_dh(b)
                turn(b - 1, dh)
                dh = following
            turn(blocks[-1], dh)
            for b in blocks:
                e, h = divmod(b, C // P)
                if e in ON_GPSIMD:
                    nc.scalar.copy(
                        out=dh_copy[e][:, h * P : (h + 1) * P, :], in_=turned[b][:].rearrange("p t c -> p c t")
                    )

        def slots_of(b):
            cols = slice(b * P % (2 * C), b * P % (2 * C) + P)
            return saved[b * P // (2 * C)][:, :, cols].rearrange("p t c -> p c t")

        def make_relu(e):
            nc.scalar.activation(
                out=relu_a[e][:].rearrange("p (c i) t -> p c t i", i=4),
                in_=saved[0][:, :, e * C : (e + 1) * C].rearrange("p t (c i) -> p c t i", i=4),
                func=RELU,
            )

        def make_da(e):
            da = stage.tile([P, C, PACK], BF16, name="g" if e == len(ON_GPSIMD) else "da", align_bytes=64)
            for h in range(C // P):
                b = e * C // P + h
                nc.vector.scalar_tensor_tensor(
                    out=da[:, h * P : (h + 1) * P, :],
                    in0=slots_of(b),
                    scalar=0.0,
                    in1=turned[b][:].rearrange("p t c -> p c t"),
                    op0=MAX,
                    op1=MULT,
                )
            products[e] = da[:].rearrange("p c t -> p (c t)")

        def quantise_da(e):
            nc.vector.quantize_mx(out=da_codes[e][:].bitcast(FP8X4), scales=da_scales[e][:], in_=products[e])

        def product_dx(e, k0, k1, on_vector=False):
            acc = ps_dx.tile([P, k1 - k0, C], F32, name="dx_acc")
            for k in range(k0, k1):
                nc.tensor.matmul_mx(
                    out=acc[:, k - k0, :],
                    lhsT=w1[e][:, 2 * k * P : 2 * (k + 1) * P].bitcast(FP4X4),
                    lhsT_scale=w1_sc[:, e, k * P : (k + 1) * P],
                    rhs=da_codes[e][:].bitcast(FP8X4),
                    rhs_scale=da_scales[e][:],
                    start=True,
                    stop=True,
                )
            slots = dx[:, k0:k1, e * C : (e + 1) * C]
            if on_vector:
                nc.vector.tensor_scalar(slots, acc[:], 2.0, None, MULT)
            else:
                nc.scalar.activation(out=slots, in_=acc[:], func=COPY, scale=2.0)

        last = len(CHUNKS) - 1
        for c in range(last + 1):
            gather(c, 0)
            if c:
                first_layer(c - 1)
            if c == 1:
                for e in ON_GPSIMD:
                    make_relu(e)
            gather(c, 1, lambda: quantise(c, 0))
        make_da(2)
        shared = stage.tile([P, len(ON_GPSIMD), C, PACK], BF16, name="g", align_bytes=64)
        for e in ON_GPSIMD:
            for h in range(C // P):
                part = slice(h * P, (h + 1) * P)
                nc.gpsimd.tensor_tensor(shared[:, e, part, :], dh_copy[e][:, part, :], relu_a[e][:, part, :], MULT)
            products[e] = shared[:, e, :, :].rearrange("p c t -> p (c t)")
        first_layer(last)
        for e in (2, 0, 3, 1, 4, 5):
            if e > 2:
                make_da(e)
            quantise_da(e)
            if e < E - 1:
                product_dx(e, 0, 2)
            else:
                product_dx(e, 0, 1, on_vector=True)
                product_dx(e, 1, 2)
        for e in (2, 0, 3, 1, 4, 5):
            product_dx(e, 2, 4)

        for k in range(K // P):
            x1 = stage.tile([P, T], F32, name="x1")
            x2 = stage.tile([P, T], F32, name="x2")
            total = stage.tile([P, T], F32, name="total")
            nc.vector.tensor_copy(x1[:], dx[:, k, :].indirect(pos1_sb[:]))
            for c0, c1 in ((0, T),) if k < K // P - 1 else ((0, T // 2), (T // 2, T)):
                nc.vector.tensor_copy(x2[:, c0:c1], dx[:, k, :].indirect(pos2_sb[:, c0 // 16 : c1 // 16]))
                adder = nc.vector if c0 else nc.gpsimd
                adder.tensor_tensor(total[:, c0:c1], x1[:, c0:c1], x2[:, c0:c1], ADD)
                nc.sync.dma_start(out=out[k * P : (k + 1) * P, c0:c1], in_=total[:, c0:c1])
